import numpy as np
import ml_dtypes


def mxq(x, axis, fmt="e4m3"):
    dtype, down = {"e4m3": (ml_dtypes.float8_e4m3fn, 7), "e5m2": (ml_dtypes.float8_e5m2, 14)}[fmt]
    v = np.moveaxis(np.asarray(x, np.float32).astype(ml_dtypes.bfloat16).astype(np.float64), axis, -1)
    blocks = v.reshape(v.shape[:-1] + (-1, 32))
    amax = np.abs(blocks).max(-1, keepdims=True)
    byte = np.maximum(np.where(amax > 0, np.frexp(amax)[1] - 1 + 127, 0) - down, 1)
    scale = np.exp2(byte - 127.0)
    codes = (blocks / scale).astype(np.float32).astype(dtype).astype(np.float64)
    return np.moveaxis((codes * scale).reshape(v.shape), -1, axis)


WIDE = False


def mx_kscale(k):
    if not WIDE:
        return np.ones(k)
    levels = np.array([10, -10, 5, -5, 0])
    if k % 512:
        return np.exp2(np.random.permutation(np.resize(levels, k // 32))).repeat(32)
    a = np.empty((k // 512, 16))
    for p in range(k // 512):
        a[p, :8] = np.random.permutation(np.resize(levels, 8))
        for g in range(8):
            far = levels[np.abs(levels - a[p, g]) >= 10]
            a[p, g + 8] = far[np.random.randint(len(far))]
    return np.exp2(a.ravel()).repeat(32)


def f64(x):
    return np.asarray(x).astype(np.float64)


def striped(idx):
    return np.tile(idx.reshape(-1, 16).T, (8, 1)).astype(np.uint16)


def unstriped(offs):
    return offs[:16].T.reshape(-1).astype(np.int64)


E2M1 = np.array([0.0, 0.5, 1.0, 1.5, 2.0, 3.0, 4.0, 6.0, -0.0, -0.5, -1.0, -1.5, -2.0, -3.0, -4.0, -6.0])


def pack_weight(w, fmt):
    k, n = w.shape
    w = f64(np.asarray(w, np.float32).astype(ml_dtypes.bfloat16)).reshape(k // 32, 32, n)
    amax = np.abs(w).max(1)
    if fmt == "e4m3":
        byte = np.frexp(amax)[1] - 1 + 127 - 7
    else:
        mant, ex = np.frexp(amax / 6.0)
        byte = np.where(mant > 0.5, ex, ex - 1) + 127
    byte = np.clip(np.where(amax > 0, byte, 1), 1, 254)
    scaled = (w * np.exp2(127.0 - byte)[:, None, :]).reshape(k, n).astype(np.float32)
    by_word = np.ascontiguousarray(scaled.reshape(k // 512, 128, 4, n).transpose(0, 1, 3, 2))
    if fmt == "e4m3":
        words = by_word.astype(ml_dtypes.float8_e4m3fn).view(np.uint8)
    else:
        c = by_word.astype(ml_dtypes.float4_e2m1fn).view(np.uint8) & 0xF
        words = (c[..., 0::2] | (c[..., 1::2] << 4)).reshape(k // 512, 128, 2 * n)
    return np.ascontiguousarray(words), np.ascontiguousarray(byte.astype(np.uint8).reshape(k // 512, 16, n))


def unpack_weight(words, scales, fmt):
    g, _, n = scales.shape
    words = np.ascontiguousarray(words).reshape(g, 128, n, -1)
    if fmt == "e4m3":
        vals = words.view(ml_dtypes.float8_e4m3fn).astype(np.float64)
    else:
        nib = np.empty((g, 128, n, 4), np.uint8)
        nib[..., 0::2] = words & 0xF
        nib[..., 1::2] = words >> 4
        vals = E2M1[nib]
    vals = vals * np.repeat(np.exp2(scales.astype(np.float64) - 127.0), 8, axis=1)[..., None]
    return vals.transpose(0, 1, 3, 2).reshape(g * 512, n)


def gelu(v):
    return 0.5 * v * (1.0 + np.tanh(np.sqrt(2.0 / np.pi) * (v + 0.044715 * v**3)))


def striped8(idx):
    return np.concatenate([v.reshape(-1, 16).T for v in idx]).astype(np.uint16)


def unstriped8(offs):
    return np.stack([offs[16 * g:16 * g + 16].T.reshape(-1) for g in range(8)]).astype(np.int64)


def runs(v, idx8):
    k = np.arange(v.shape[0])
    return v[k[:, None], idx8[k % 512 // 64]]


K, K2, H, N, T, S, T2 = 1024, 512, 1024, 512, 2048, 1024, 2048


def setup_inputs():
    n = np.random.standard_normal
    s = mx_kscale(K)[:, None]
    s2 = mx_kscale(K2)[:, None]
    u = mx_kscale(H)[:, None]
    tab_words, tab_scales = pack_weight(n((K, T)) * s, "e4m3")
    tab2_words, tab2_scales = pack_weight(n((K2, T)) * s2, "e4m3")
    w2_words, w2_scales = pack_weight(n((K2, H)) / np.sqrt(K2) / s2 * u.T, "e2m1")
    return {
        "tab_words": tab_words, "tab_scales": tab_scales,
        "offs": striped8(np.stack([np.random.permutation(T)[:S] for _ in range(8)])),
        "w1": (0.4 * n((K, H)) / np.sqrt(K) / s).astype(np.float32),
        "ph": np.random.uniform(-1.0, 1.0, H).astype(np.float32),
        "tab2_words": tab2_words, "tab2_scales": tab2_scales,
        "offs2": striped(np.random.permutation(T)[:S]),
        "w2_words": w2_words, "w2_scales": w2_scales,
        "w3": (1.2 * n((H, N)) / np.sqrt(H) / u).astype(np.float32),
        "offs3": striped(np.random.permutation(T2)[:S]),
        "wgo": np.exp(0.3 * n((128, S))).astype(np.float32),
        "page1": n((N, T2)).astype(np.float32),
    }


def reference(tab_words, tab_scales, offs, w1, ph, tab2_words, tab2_scales, offs2,
              w2_words, w2_scales, w3, offs3, wgo, page1):
    v = runs(unpack_weight(tab_words, tab_scales, "e4m3"), unstriped8(offs))
    v2 = unpack_weight(tab2_words, tab2_scales, "e4m3")[:, unstriped(offs2)]
    a = mxq(f64(w1), 0, "e4m3").T @ v
    b = unpack_weight(w2_words, w2_scales, "e2m1").T @ v2
    z = np.cos(a + f64(ph)[:, None]) * np.abs(b)
    y = mxq(f64(w3), 0, "e4m3").T @ mxq(z, 0, "e4m3")
    out = f64(page1).copy()
    out[:, unstriped(offs3)] = np.tile(f64(wgo), (N // 128, 1)) * y
    return out

@@ -1,0 +1,257 @@
+import math
+from contextlib import ExitStack
+
+import concourse.mybir as mybir
+
+K, K2, H, N, T, S, T2 = 1024, 512, 1024, 512, 2048, 1024, 2048
+FLOPS = 2 * S * (K * H + K2 * H + H * N)
+
+F32 = mybir.dt.float32
+BF16 = mybir.dt.bfloat16
+I32 = mybir.dt.int32
+U32 = mybir.dt.uint32
+U16 = mybir.dt.uint16
+U8 = mybir.dt.uint8
+FP8X4 = mybir.dt.float8_e4m3fn_x4
+FP4X4 = mybir.dt.float4_e2m1fn_x4
+ACT = mybir.ActivationFunctionType
+ALU = mybir.AluOpType
+
+P = 128
+PACK = 4
+KP = P * PACK
+SL = 256
+NS = S // SL
+GW = 512
+
+
+def tile_list_paired_beat_scores_kernel(
+    tc, tab_words, tab_scales, offs, w1, ph, tab2_words, tab2_scales, offs2,
+    w2_words, w2_scales, w3, offs3, wgo, page1, out,
+):
+    nc = tc.nc
+    with ExitStack() as ctx:
+        keep = ctx.enter_context(tc.tile_pool(name="keep", bufs=1))
+        work = ctx.enter_context(tc.tile_pool(name="work", bufs=2))
+        big = ctx.enter_context(tc.tile_pool(name="big", bufs=6))
+        psum = ctx.enter_context(tc.psum_pool(name="psum", bufs=1))
+
+        def held(shape, dtype, name):
+            return keep.tile(shape, dtype, name=name, align_bytes=64)
+
+        list1 = keep.tile([P, S // 16], U16, name="list1")
+        list2 = keep.tile([P, S // 16], U16, name="list2")
+        list3 = keep.tile([P, S // 16], U16, name="list3")
+        def staged(shape, dtype):
+            return big.tile(shape, dtype, name="big", align_bytes=64)
+
+        def streamed(shape, dtype, src):
+            t = staged(shape, dtype)
+            dst = t[:] if dtype == F32 else t[:].bitcast(I32)
+            nc.sync.dma_start(out=dst, in_=src)
+            return t
+
+        def load_words(ap):
+            return streamed([P, T], U32, ap.rearrange("p t i -> p (t i)").bitcast(I32))
+
+        def load_rows(ap):
+            return streamed([P, PACK, KP], F32, ap.rearrange("(p j) c -> p j c", j=PACK))
+
+        nc.sync.dma_start(list1[:], offs)
+        nc.sync.dma_start(list2[:], offs2)
+        nc.sync.dma_start(list3[:], offs3)
+        ph_sb = streamed([P, 2, PACK], F32, ph.rearrange("(b p t) -> p b t", b=2, t=PACK))
+        tab2_w = load_words(tab2_words[0])
+        w2_raw = streamed([P, 2 * H], U8, w2_words[0].bitcast(I32))
+        w1_raw = {}
+        w1_raw[0, 0] = load_rows(w1[0:KP, 0:KP])
+        tab_s = staged([P, T], U8)
+        tab2_s = staged([P, T], U8)
+        w2_sraw = held([P, H], U8, "w2_sraw")
+        nc.gpsimd.memset(w2_sraw[:].bitcast(I32), 0)
+        nc.vector.memset(tab_s[:].bitcast(I32), 0)
+        nc.vector.memset(tab2_s[:].bitcast(I32), 0)
+        for d in range(4):
+            nc.gpsimd.dma_start(
+                out=w2_sraw[32 * d:32 * d + 4, :].bitcast(I32),
+                in_=w2_scales[0, 4 * d:4 * d + 4, :].bitcast(I32),
+            )
+        for r in range(2):
+            nc.scalar.dma_start(
+                out=tab_s[r:P:8, :].bitcast(I32),
+                in_=tab_scales[:, r:16:2, :].bitcast(I32).rearrange("a g t -> g a t"),
+            )
+        for d in range(4):
+            nc.scalar.dma_start(
+                out=tab2_s[32 * d:32 * d + 4, :].bitcast(I32),
+                in_=tab2_scales[0, 4 * d:4 * d + 4, :].bitcast(I32),
+            )
+        w1_raw[1, 0] = load_rows(w1[KP:2 * KP, 0:KP])
+        tab_w = [load_words(tab_words[a]) for a in range(2)]
+        for a in range(2):
+            w1_raw[a, 1] = load_rows(w1[a * KP:(a + 1) * KP, KP:2 * KP])
+        w3_raw = [load_rows(w3[b * KP:(b + 1) * KP, :]) for b in range(2)]
+        wgo_sb = streamed([P, S], F32, wgo)
+        page = [streamed([P, T2], F32, page1[n * P:(n + 1) * P, :]) for n in range(N // P)]
+
+        v_sg = held([P, S], U8, "v_sg")
+        v_s = held([P, S], U8, "v_s")
+        v2_s = held([P, S], U8, "v2_s")
+
+        half_ph = held([P, 2 * PACK], F32, "half_ph")
+        nc.vector.tensor_scalar(half_ph[:], ph_sb[:].rearrange("p b t -> p (b t)"), 0.5, None, ALU.mult)
+
+        w2_c = held([P, 2 * H], U8, "w2_c")
+        w2_s = held([P, H], U8, "w2_s")
+        nc.scalar.copy(
+            out=w2_c[:].bitcast(U16).rearrange("p (b t m) -> p b t m", b=2, t=PACK),
+            in_=w2_raw[:].bitcast(U16).rearrange("p (b m t) -> p b t m", b=2, t=PACK),
+        )
+
+        v_w = [[held([P, GW], U32, f"v_w{a}{h}") for h in range(S // GW)] for a in range(2)]
+        v2_w = [held([P, GW], U32, f"v2_w{h}") for h in range(S // GW)]
+
+        def gather_words(dst, window, lst, h):
+            nc.vector.tensor_copy(dst[:], window[:].indirect(lst[:, h * GW // 16:(h + 1) * GW // 16]))
+
+        def cast(eng, dst, src):
+            if eng == "s":
+                nc.scalar.copy(out=dst, in_=src)
+            else:
+                nc.vector.tensor_copy(out=dst, in_=src)
+
+        w1_c = [[held([P, KP], U32, f"w1_c{a}{b}") for b in range(2)] for a in range(2)]
+        w1_s = [[held([P, KP], U8, f"w1_s{a}{b}") for b in range(2)] for a in range(2)]
+        w3_c = [held([P, N], U32, f"w3_c{b}") for b in range(2)]
+        w3_s = [held([P, N], U8, f"w3_s{b}") for b in range(2)]
+
+        def prep_w1(a, b, eng):
+            g = work.tile([P, KP * PACK], BF16, name="g", bufs=3, align_bytes=64)
+            cast(eng, g[:].rearrange("p (t m j) -> p m t j", t=PACK, j=PACK),
+                 w1_raw[a, b][:].rearrange("p j (m t) -> p m t j", t=PACK))
+            nc.vector.quantize_mx(out=w1_c[a][b][:].bitcast(FP8X4), scales=w1_s[a][b][:], in_=g[:])
+
+        def prep_w3(b, eng):
+            g = work.tile([P, N * PACK], BF16, name="g", bufs=3, align_bytes=64)
+            cast(eng, g[:].rearrange("p (c i j) -> p c j i", i=4, j=PACK),
+                 w3_raw[b][:].rearrange("p j (c i) -> p c j i", i=4))
+            nc.vector.quantize_mx(out=w3_c[b][:].bitcast(FP8X4), scales=w3_s[b][:], in_=g[:])
+
+        def magnitudes(b, s):
+            h, c0 = divmod(s * SL, GW)
+            j0 = s * SL
+            mag = work.tile([P, SL * PACK], F32, name="mag", bufs=8)
+            for u in range(SL // P):
+                acc = psum.tile([P, PACK, P], F32, name="acc_b", bufs=2)
+                for t in range(PACK):
+                    r0 = b * KP + t * P
+                    nc.tensor.matmul_mx(
+                        out=acc[:, t, :],
+                        lhsT=w2_c[:, 2 * r0:2 * (r0 + P)].bitcast(FP4X4),
+                        lhsT_scale=w2_s[:, r0:r0 + P],
+                        rhs=v2_w[h][:, c0 + u * P:c0 + (u + 1) * P].bitcast(FP8X4),
+                        rhs_scale=v2_s[:, j0 + u * P:j0 + (u + 1) * P],
+                        start=True, stop=True,
+                    )
+                nc.scalar.activation(
+                    mag[:, u * KP:(u + 1) * KP].rearrange("p (n t) -> p n t", t=PACK),
+                    acc[:].rearrange("p t n -> p n t"), ACT.Abs)
+            return mag
+
+        def features(b, s):
+            mag = magnitudes(b, s)
+            h, c0 = divmod(s * SL, GW)
+            j0 = s * SL
+            sn = work.tile([P, PACK, SL], F32, name="sn")
+            for u in range(2):
+                acc = psum.tile([P, 2, SL], F32, name="acc_a", bufs=4)
+                for i in range(2):
+                    t = 2 * u + i
+                    for a in range(2):
+                        nc.tensor.matmul_mx(
+                            out=acc[:, i, :],
+                            lhsT=w1_c[a][b][:, t * P:(t + 1) * P].bitcast(FP8X4),
+                            lhsT_scale=w1_s[a][b][:, t * P:(t + 1) * P],
+                            rhs=v_w[a][h][:, c0:c0 + SL].bitcast(FP8X4),
+                            rhs_scale=v_s[8 * a:P, j0:j0 + SL],
+                            start=(a == 0), stop=(a == 1),
+                        )
+                for i in range(2):
+                    t = 2 * u + i
+                    nc.scalar.activation(sn[:, t, :], acc[:, i, :], ACT.Sin,
+                                         bias=half_ph[:, PACK * b + t:PACK * b + t + 1], scale=0.5)
+            sq = work.tile([P, SL * PACK], F32, name="sq", bufs=4)
+            nc.scalar.activation(sq[:].rearrange("p (c i t) -> p c t i", i=4, t=PACK),
+                                 sn[:].rearrange("p t (c i) -> p c t i", i=4), ACT.Square, scale=math.sqrt(2.0))
+            zb = work.tile([P, SL * PACK], BF16, name="zb", align_bytes=64)
+            nc.vector.scalar_tensor_tensor(zb[:], sq[:], 1.0, mag[:], ALU.subtract, ALU.mult)
+            z_c = work.tile([P, SL], U32, name="z_c", bufs=8, align_bytes=64)
+            z_s = work.tile([P, SL], U8, name="z_s", bufs=8, align_bytes=64)
+            nc.vector.quantize_mx(out=z_c[:].bitcast(FP8X4), scales=z_s[:], in_=zb[:])
+            return z_c, z_s
+
+        def scores(s, z):
+            j0 = s * SL
+            ys = []
+            for u in range(2):
+                acc = psum.tile([P, 2, SL], F32, name="acc_y", bufs=2)
+                for i in range(2):
+                    n = 2 * u + i
+                    for b in range(2):
+                        nc.tensor.matmul_mx(
+                            out=acc[:, i, :],
+                            lhsT=w3_c[b][:, n * P:(n + 1) * P].bitcast(FP8X4),
+                            lhsT_scale=w3_s[b][:, n * P:(n + 1) * P],
+                            rhs=z[b][0][:].bitcast(FP8X4),
+                            rhs_scale=z[b][1][:],
+                            start=(b == 0), stop=(b == 1),
+                        )
+                y = work.tile([P, 2, SL], F32, name="y", bufs=8)
+                nc.scalar.activation(y[:], acc[:], ACT.Copy, scale=-1.0)
+                ys.append(y)
+            for n in range(N // P):
+                nc.vector.tensor_tensor(
+                    page[n][:].indirect(list3[:, j0 // 16:(j0 + SL) // 16]),
+                    ys[n // 2][:, n % 2, :], wgo_sb[:, j0:j0 + SL], ALU.mult)
+
+        for h in range(S // GW):
+            gather_words(v2_w[h], tab2_w, list2, h)
+        nc.vector.tensor_copy(v_sg[:], tab_s[:].indirect(list1[:]))
+        nc.vector.tensor_copy(v_s[:].bitcast(I32), v_sg[:].bitcast(I32))
+        for a in range(2):
+            for r in range(2):
+                nc.scalar.dma_start(
+                    out=v_s[8 * a + 2 + r:P:32, :].bitcast(I32),
+                    in_=v_sg[16 + 8 * a + r:P:32, :].bitcast(I32),
+                )
+        nc.vector.tensor_copy(v2_s[:], tab2_s[:].indirect(list2[:]))
+        nc.vector.tensor_copy(
+            out=w2_s[:].rearrange("p (b t m) -> p b t m", b=2, t=PACK),
+            in_=w2_sraw[:].rearrange("p (b m t) -> p b t m", b=2, t=PACK),
+        )
+
+        prep_w1(0, 0, "s")
+        prep_w1(1, 0, "s")
+        gather_words(v_w[0][0], tab_w[0], list1, 0)
+        gather_words(v_w[1][0], tab_w[1], list1, 0)
+        gather_words(v_w[0][1], tab_w[0], list1, 1)
+        gather_words(v_w[1][1], tab_w[1], list1, 1)
+        z = {}
+        z[0, 0] = features(0, 0)
+        prep_w1(0, 1, "v")
+        prep_w1(1, 1, "v")
+        z[0, 1] = features(0, 1)
+        prep_w3(0, "s")
+        prep_w3(1, "v")
+        z[1, 0] = features(1, 0)
+        z[1, 1] = features(1, 1)
+        scores(0, [z[0, 0], z[1, 0]])
+        z[0, 2] = features(0, 2)
+        z[1, 2] = features(1, 2)
+        scores(1, [z[0, 1], z[1, 1]])
+        z[0, 3] = features(0, 3)
+        z[1, 3] = features(1, 3)
+        scores(2, [z[0, 2], z[1, 2]])
+        scores(3, [z[0, 3], z[1, 3]])
+        for n in range(N // P):
+            nc.sync.dma_start(out=out[n * P:(n + 1) * P, :], in_=page[n][:])

@@ -23,6 +23,7 @@ KP = P * PACK
 SL = 256
 NS = S // SL
 GW = 512
+BANK = 2048
 
 
 def tile_list_paired_beat_scores_kernel(
@@ -33,7 +34,7 @@ def tile_list_paired_beat_scores_kernel(
     with ExitStack() as ctx:
         keep = ctx.enter_context(tc.tile_pool(name="keep", bufs=1))
         work = ctx.enter_context(tc.tile_pool(name="work", bufs=2))
-        big = ctx.enter_context(tc.tile_pool(name="big", bufs=6))
+        big = ctx.enter_context(tc.tile_pool(name="big", bufs=1))
         psum = ctx.enter_context(tc.psum_pool(name="psum", bufs=1))
 
         def held(shape, dtype, name):
@@ -42,40 +43,35 @@ def tile_list_paired_beat_scores_kernel(
         list1 = keep.tile([P, S // 16], U16, name="list1")
         list2 = keep.tile([P, S // 16], U16, name="list2")
         list3 = keep.tile([P, S // 16], U16, name="list3")
-        def staged(shape, dtype):
-            return big.tile(shape, dtype, name="big", align_bytes=64)
+        def staged(kib, name, shape, dtype):
+            return big.tile(shape, dtype, name=name, align_bytes=64, offset=kib * 1024)
 
-        def streamed(shape, dtype, src):
-            t = staged(shape, dtype)
+        def streamed(kib, name, shape, dtype, src):
+            t = staged(kib, name, shape, dtype)
             dst = t[:] if dtype == F32 else t[:].bitcast(I32)
             nc.sync.dma_start(out=dst, in_=src)
             return t
 
-        def load_words(ap):
-            return streamed([P, T], U32, ap.rearrange("p t i -> p (t i)").bitcast(I32))
+        def load_words(kib, name, ap):
+            return streamed(kib, name, [P, T], U32, ap.rearrange("p t i -> p (t i)").bitcast(I32))
 
-        def load_rows(ap):
-            return streamed([P, PACK, KP], F32, ap.rearrange("(p j) c -> p j c", j=PACK))
+        def load_rows(kib, name, ap):
+            return streamed(kib, name, [P, PACK, KP], F32, ap.rearrange("(p j) c -> p j c", j=PACK))
 
         nc.sync.dma_start(list1[:], offs)
         nc.sync.dma_start(list2[:], offs2)
         nc.sync.dma_start(list3[:], offs3)
-        ph_sb = streamed([P, 2, PACK], F32, ph.rearrange("(b p t) -> p b t", b=2, t=PACK))
-        tab2_w = load_words(tab2_words[0])
-        w2_raw = streamed([P, 2 * H], U8, w2_words[0].bitcast(I32))
+        ph_sb = streamed(20, "ph_sb", [P, 2, PACK], F32, ph.rearrange("(b p t) -> p b t", b=2, t=PACK))
+        tab_w = {}
         w1_raw = {}
-        w1_raw[0, 0] = load_rows(w1[0:KP, 0:KP])
-        tab_s = staged([P, T], U8)
-        tab2_s = staged([P, T], U8)
+        tab_w[0] = load_words(36, "tab_w0", tab_words[0])
+        w1_raw[0, 0] = load_rows(4, "w1_00", w1[0:KP, 0:KP])
+        tab_s = staged(44, "tab_s", [P, T], U8)
+        tab2_s = staged(53, "tab2_s", [P, T], U8)
         w2_sraw = held([P, H], U8, "w2_sraw")
-        nc.gpsimd.memset(w2_sraw[:].bitcast(I32), 0)
         nc.vector.memset(tab_s[:].bitcast(I32), 0)
         nc.vector.memset(tab2_s[:].bitcast(I32), 0)
-        for d in range(4):
-            nc.gpsimd.dma_start(
-                out=w2_sraw[32 * d:32 * d + 4, :].bitcast(I32),
-                in_=w2_scales[0, 4 * d:4 * d + 4, :].bitcast(I32),
-            )
+        nc.vector.memset(w2_sraw[:].bitcast(I32), 0)
         for r in range(2):
             nc.scalar.dma_start(
                 out=tab_s[r:P:8, :].bitcast(I32),
@@ -86,13 +82,20 @@ def tile_list_paired_beat_scores_kernel(
                 out=tab2_s[32 * d:32 * d + 4, :].bitcast(I32),
                 in_=tab2_scales[0, 4 * d:4 * d + 4, :].bitcast(I32),
             )
-        w1_raw[1, 0] = load_rows(w1[KP:2 * KP, 0:KP])
-        tab_w = [load_words(tab_words[a]) for a in range(2)]
+        for d in range(4):
+            nc.scalar.dma_start(
+                out=w2_sraw[32 * d:32 * d + 4, :].bitcast(I32),
+                in_=w2_scales[0, 4 * d:4 * d + 4, :].bitcast(I32),
+            )
+        w1_raw[1, 0] = load_rows(20, "w1_10", w1[KP:2 * KP, 0:KP])
+        tab_w[1] = load_words(44, "tab_w1", tab_words[1])
+        w2_raw = streamed(52, "w2_raw", [P, 2 * H], U8, w2_words[0].bitcast(I32))
+        tab2_w = load_words(54, "tab2_w", tab2_words[0])
         for a in range(2):
-            w1_raw[a, 1] = load_rows(w1[a * KP:(a + 1) * KP, KP:2 * KP])
-        w3_raw = [load_rows(w3[b * KP:(b + 1) * KP, :]) for b in range(2)]
-        wgo_sb = streamed([P, S], F32, wgo)
-        page = [streamed([P, T2], F32, page1[n * P:(n + 1) * P, :]) for n in range(N // P)]
+            w1_raw[a, 1] = load_rows(8 * a, f"w1_{a}1", w1[a * KP:(a + 1) * KP, KP:2 * KP])
+        w3_raw = [load_rows(16 + 8 * b, f"w3_{b}", w3[b * KP:(b + 1) * KP, :]) for b in range(2)]
+        wgo_sb = streamed(0, "wgo_sb", [P, S], F32, wgo)
+        page = [streamed(4 + 8 * n, f"page{n}", [P, T2], F32, page1[n * P:(n + 1) * P, :]) for n in range(N // P)]
 
         v_sg = held([P, S], U8, "v_sg")
         v_s = held([P, S], U8, "v_s")
@@ -102,14 +105,15 @@ def tile_list_paired_beat_scores_kernel(
         nc.vector.tensor_scalar(half_ph[:], ph_sb[:].rearrange("p b t -> p (b t)"), 0.5, None, ALU.mult)
 
         w2_c = held([P, 2 * H], U8, "w2_c")
-        w2_s = held([P, H], U8, "w2_s")
+        w2_s = staged(36, "w2_s", [P, H], U8)
         nc.scalar.copy(
             out=w2_c[:].bitcast(U16).rearrange("p (b t m) -> p b t m", b=2, t=PACK),
             in_=w2_raw[:].bitcast(U16).rearrange("p (b m t) -> p b t m", b=2, t=PACK),
         )
 
-        v_w = [[held([P, GW], U32, f"v_w{a}{h}") for h in range(S // GW)] for a in range(2)]
-        v2_w = [held([P, GW], U32, f"v2_w{h}") for h in range(S // GW)]
+        v_w = [[held([P, GW], U32, "v_w00"), held([P, GW], U32, "v_w01")],
+               [held([P, GW], U32, "v_w10"), staged(99, "v_w11", [P, GW], U32)]]
+        v2_w = [staged(101, "v2_w0", [P, GW], U32), staged(103, "v2_w1", [P, GW], U32)]
 
         def gather_words(dst, window, lst, h):
             nc.vector.tensor_copy(dst[:], window[:].indirect(lst[:, h * GW // 16:(h + 1) * GW // 16]))
@@ -126,23 +130,29 @@ def tile_list_paired_beat_scores_kernel(
         w3_s = [held([P, N], U8, f"w3_s{b}") for b in range(2)]
 
         def prep_w1(a, b, eng):
-            g = work.tile([P, KP * PACK], BF16, name="g", bufs=3, align_bytes=64)
+            g = staged(96 + 4 * a + 10 * b, f"w1_g{a}{b}", [P, KP * PACK], BF16)
             cast(eng, g[:].rearrange("p (t m j) -> p m t j", t=PACK, j=PACK),
                  w1_raw[a, b][:].rearrange("p j (m t) -> p m t j", t=PACK))
             nc.vector.quantize_mx(out=w1_c[a][b][:].bitcast(FP8X4), scales=w1_s[a][b][:], in_=g[:])
 
         def prep_w3(b, eng):
-            g = work.tile([P, N * PACK], BF16, name="g", bufs=3, align_bytes=64)
+            g = staged(114 + 4 * b, f"w3_g{b}", [P, N * PACK], BF16)
             cast(eng, g[:].rearrange("p (c i j) -> p c j i", i=4, j=PACK),
                  w3_raw[b][:].rearrange("p j (c i) -> p c j i", i=4))
             nc.vector.quantize_mx(out=w3_c[b][:].bitcast(FP8X4), scales=w3_s[b][:], in_=g[:])
 
+        def a_bank(b, s):
+            return 0 if b + s == 0 else 2 if b == 1 or s == 1 else 4
+
+        def sn_at(b, s):
+            return (64 + 4 * (2 * s + b)) * 1024
+
         def magnitudes(b, s):
             h, c0 = divmod(s * SL, GW)
             j0 = s * SL
-            mag = work.tile([P, SL * PACK], F32, name="mag", bufs=8)
+            mag = work.tile([P, SL * PACK], F32, name="mag", bufs=3)
             for u in range(SL // P):
-                acc = psum.tile([P, PACK, P], F32, name="acc_b", bufs=2)
+                acc = psum.tile([P, PACK, P], F32, name=f"acc_b{b}{s}{u}", offset=u * BANK)
                 for t in range(PACK):
                     r0 = b * KP + t * P
                     nc.tensor.matmul_mx(
@@ -159,12 +169,11 @@ def tile_list_paired_beat_scores_kernel(
             return mag
 
         def features(b, s):
-            mag = magnitudes(b, s)
             h, c0 = divmod(s * SL, GW)
             j0 = s * SL
-            sn = work.tile([P, PACK, SL], F32, name="sn")
+            sn = big.tile([P, PACK, SL], F32, name=f"sn{b}{s}", offset=sn_at(b, s))
             for u in range(2):
-                acc = psum.tile([P, 2, SL], F32, name="acc_a", bufs=4)
+                acc = psum.tile([P, 2, SL], F32, name=f"acc_a{b}{s}{u}", offset=(a_bank(b, s) + u) * BANK)
                 for i in range(2):
                     t = 2 * u + i
                     for a in range(2):
@@ -183,6 +192,7 @@ def tile_list_paired_beat_scores_kernel(
             sq = work.tile([P, SL * PACK], F32, name="sq", bufs=4)
             nc.scalar.activation(sq[:].rearrange("p (c i t) -> p c t i", i=4, t=PACK),
                                  sn[:].rearrange("p t (c i) -> p c t i", i=4), ACT.Square, scale=math.sqrt(2.0))
+            mag = magnitudes(b, s)
             zb = work.tile([P, SL * PACK], BF16, name="zb", align_bytes=64)
             nc.vector.scalar_tensor_tensor(zb[:], sq[:], 1.0, mag[:], ALU.subtract, ALU.mult)
             z_c = work.tile([P, SL], U32, name="z_c", bufs=8, align_bytes=64)
@@ -190,68 +200,66 @@ def tile_list_paired_beat_scores_kernel(
             nc.vector.quantize_mx(out=z_c[:].bitcast(FP8X4), scales=z_s[:], in_=zb[:])
             return z_c, z_s
 
-        def scores(s, z):
-            j0 = s * SL
-            ys = []
-            for u in range(2):
-                acc = psum.tile([P, 2, SL], F32, name="acc_y", bufs=2)
-                for i in range(2):
-                    n = 2 * u + i
-                    for b in range(2):
-                        nc.tensor.matmul_mx(
-                            out=acc[:, i, :],
-                            lhsT=w3_c[b][:, n * P:(n + 1) * P].bitcast(FP8X4),
-                            lhsT_scale=w3_s[b][:, n * P:(n + 1) * P],
-                            rhs=z[b][0][:].bitcast(FP8X4),
-                            rhs_scale=z[b][1][:],
-                            start=(b == 0), stop=(b == 1),
-                        )
-                y = work.tile([P, 2, SL], F32, name="y", bufs=8)
-                nc.scalar.activation(y[:], acc[:], ACT.Copy, scale=-1.0)
-                ys.append(y)
-            for n in range(N // P):
+        def scores(items, z, bank, y_at):
+            acc = psum.tile([P, 2, SL], F32, name=f"acc_y{items[0]}", offset=bank * BANK)
+            for i, (n, s) in enumerate(items):
+                for b in range(2):
+                    nc.tensor.matmul_mx(
+                        out=acc[:, i, :],
+                        lhsT=w3_c[b][:, n * P:(n + 1) * P].bitcast(FP8X4),
+                        lhsT_scale=w3_s[b][:, n * P:(n + 1) * P],
+                        rhs=z[b, s][0][:].bitcast(FP8X4),
+                        rhs_scale=z[b, s][1][:],
+                        start=(b == 0), stop=(b == 1),
+                    )
+            y = big.tile([P, 2, SL], F32, name=f"y{items[0]}", offset=y_at)
+            nc.scalar.activation(y[:], acc[:], ACT.Copy, scale=-1.0)
+            for i, (n, s) in enumerate(items):
+                j0 = s * SL
                 nc.vector.tensor_tensor(
                     page[n][:].indirect(list3[:, j0 // 16:(j0 + SL) // 16]),
-                    ys[n // 2][:, n % 2, :], wgo_sb[:, j0:j0 + SL], ALU.mult)
+                    y[:, i, :], wgo_sb[:, j0:j0 + SL], ALU.mult)
 
-        for h in range(S // GW):
-            gather_words(v2_w[h], tab2_w, list2, h)
         nc.vector.tensor_copy(v_sg[:], tab_s[:].indirect(list1[:]))
         nc.vector.tensor_copy(v_s[:].bitcast(I32), v_sg[:].bitcast(I32))
         for a in range(2):
             for r in range(2):
-                nc.scalar.dma_start(
+                nc.gpsimd.dma_start(
                     out=v_s[8 * a + 2 + r:P:32, :].bitcast(I32),
                     in_=v_sg[16 + 8 * a + r:P:32, :].bitcast(I32),
                 )
         nc.vector.tensor_copy(v2_s[:], tab2_s[:].indirect(list2[:]))
+        gather_words(v_w[0][0], tab_w[0], list1, 0)
+        prep_w1(0, 0, "s")
+        gather_words(v_w[0][1], tab_w[0], list1, 1)
         nc.vector.tensor_copy(
             out=w2_s[:].rearrange("p (b t m) -> p b t m", b=2, t=PACK),
             in_=w2_sraw[:].rearrange("p (b m t) -> p b t m", b=2, t=PACK),
         )
 
-        prep_w1(0, 0, "s")
         prep_w1(1, 0, "s")
-        gather_words(v_w[0][0], tab_w[0], list1, 0)
         gather_words(v_w[1][0], tab_w[1], list1, 0)
-        gather_words(v_w[0][1], tab_w[0], list1, 1)
         gather_words(v_w[1][1], tab_w[1], list1, 1)
-        z = {}
-        z[0, 0] = features(0, 0)
+        gather_words(v2_w[0], tab2_w, list2, 0)
+        gather_words(v2_w[1], tab2_w, list2, 1)
         prep_w1(0, 1, "v")
         prep_w1(1, 1, "v")
+        z = {}
+        z[0, 0] = features(0, 0)
         z[0, 1] = features(0, 1)
-        prep_w3(0, "s")
+        prep_w3(0, "v")
         prep_w3(1, "v")
         z[1, 0] = features(1, 0)
-        z[1, 1] = features(1, 1)
-        scores(0, [z[0, 0], z[1, 0]])
-        z[0, 2] = features(0, 2)
-        z[1, 2] = features(1, 2)
-        scores(1, [z[0, 1], z[1, 1]])
-        z[0, 3] = features(0, 3)
-        z[1, 3] = features(1, 3)
-        scores(2, [z[0, 2], z[1, 2]])
-        scores(3, [z[0, 3], z[1, 3]])
+        for s in range(1, NS):
+            if s > 1:
+                z[0, s] = features(0, s)
+            z[1, s] = features(1, s)
+            scores([(0, s - 1), (1, s - 1)], z, a_bank(1, s), sn_at(1, s))
+            if s < NS - 1:
+                scores([(2, s - 1), (3, s - 1)], z, a_bank(1, s) + 1, sn_at(1, s) + 2048)
+        last = NS - 1
+        scores([(0, last), (1, last)], z, a_bank(1, last) + 1, sn_at(1, last) + 2048)
+        scores([(2, last), (2, last - 1)], z, a_bank(1, last), sn_at(0, last))
+        scores([(3, last), (3, last - 1)], z, a_bank(1, last) + 1, sn_at(0, last) + 2048)
         for n in range(N // P):
             nc.sync.dma_start(out=out[n * P:(n + 1) * P, :], in_=page[n][:])

import math
from contextlib import ExitStack

import concourse.mybir as mybir

K, K2, H, N, T, S, T2 = 1024, 512, 1024, 512, 2048, 1024, 2048
FLOPS = 2 * S * (K * H + K2 * H + H * N)

F32 = mybir.dt.float32
BF16 = mybir.dt.bfloat16
I32 = mybir.dt.int32
U32 = mybir.dt.uint32
U16 = mybir.dt.uint16
U8 = mybir.dt.uint8
FP8X4 = mybir.dt.float8_e4m3fn_x4
FP4X4 = mybir.dt.float4_e2m1fn_x4
ACT = mybir.ActivationFunctionType
ALU = mybir.AluOpType

P = 128
PACK = 4
KP = P * PACK
SL = 256
NS = S // SL
GW = 512
BANK = 2048


def tile_list_paired_beat_scores_kernel(
    tc, tab_words, tab_scales, offs, w1, ph, tab2_words, tab2_scales, offs2,
    w2_words, w2_scales, w3, offs3, wgo, page1, out,
):
    nc = tc.nc
    with ExitStack() as ctx:
        keep = ctx.enter_context(tc.tile_pool(name="keep", bufs=1))
        work = ctx.enter_context(tc.tile_pool(name="work", bufs=2))
        big = ctx.enter_context(tc.tile_pool(name="big", bufs=1))
        psum = ctx.enter_context(tc.psum_pool(name="psum", bufs=1))

        def held(shape, dtype, name):
            return keep.tile(shape, dtype, name=name, align_bytes=64)

        list1 = keep.tile([P, S // 16], U16, name="list1")
        list2 = keep.tile([P, S // 16], U16, name="list2")
        list3 = keep.tile([P, S // 16], U16, name="list3")
        def staged(kib, name, shape, dtype):
            return big.tile(shape, dtype, name=name, align_bytes=64, offset=kib * 1024)

        def streamed(kib, name, shape, dtype, src):
            t = staged(kib, name, shape, dtype)
            dst = t[:] if dtype == F32 else t[:].bitcast(I32)
            nc.sync.dma_start(out=dst, in_=src)
            return t

        def load_words(kib, name, ap):
            return streamed(kib, name, [P, T], U32, ap.rearrange("p t i -> p (t i)").bitcast(I32))

        def load_rows(kib, name, ap):
            return streamed(kib, name, [P, PACK, KP], F32, ap.rearrange("(p j) c -> p j c", j=PACK))

        nc.sync.dma_start(list1[:], offs)
        nc.sync.dma_start(list2[:], offs2)
        nc.sync.dma_start(list3[:], offs3)
        ph_sb = streamed(20, "ph_sb", [P, 2, PACK], F32, ph.rearrange("(b p t) -> p b t", b=2, t=PACK))
        tab_w = {}
        w1_raw = {}
        tab_w[0] = load_words(36, "tab_w0", tab_words[0])
        w1_raw[0, 0] = load_rows(4, "w1_00", w1[0:KP, 0:KP])
        tab_s = staged(44, "tab_s", [P, T], U8)
        tab2_s = staged(53, "tab2_s", [P, T], U8)
        w2_sraw = held([P, H], U8, "w2_sraw")
        nc.vector.memset(tab_s[:].bitcast(I32), 0)
        nc.vector.memset(tab2_s[:].bitcast(I32), 0)
        nc.vector.memset(w2_sraw[:].bitcast(I32), 0)
        for r in range(2):
            nc.scalar.dma_start(
                out=tab_s[r:P:8, :].bitcast(I32),
                in_=tab_scales[:, r:16:2, :].bitcast(I32).rearrange("a g t -> g a t"),
            )
        for d in range(4):
            nc.scalar.dma_start(
                out=tab2_s[32 * d:32 * d + 4, :].bitcast(I32),
                in_=tab2_scales[0, 4 * d:4 * d + 4, :].bitcast(I32),
            )
        for d in range(4):
            nc.scalar.dma_start(
                out=w2_sraw[32 * d:32 * d + 4, :].bitcast(I32),
                in_=w2_scales[0, 4 * d:4 * d + 4, :].bitcast(I32),
            )
        w1_raw[1, 0] = load_rows(20, "w1_10", w1[KP:2 * KP, 0:KP])
        tab_w[1] = load_words(44, "tab_w1", tab_words[1])
        w2_raw = streamed(52, "w2_raw", [P, 2 * H], U8, w2_words[0].bitcast(I32))
        tab2_w = load_words(54, "tab2_w", tab2_words[0])
        for a in range(2):
            w1_raw[a, 1] = load_rows(8 * a, f"w1_{a}1", w1[a * KP:(a + 1) * KP, KP:2 * KP])
        w3_raw = [load_rows(16 + 8 * b, f"w3_{b}", w3[b * KP:(b + 1) * KP, :]) for b in range(2)]
        wgo_sb = streamed(0, "wgo_sb", [P, S], F32, wgo)
        page = [streamed(4 + 8 * n, f"page{n}", [P, T2], F32, page1[n * P:(n + 1) * P, :]) for n in range(N // P)]

        v_sg = held([P, S], U8, "v_sg")
        v_s = held([P, S], U8, "v_s")
        v2_s = held([P, S], U8, "v2_s")

        half_ph = held([P, 2 * PACK], F32, "half_ph")
        nc.vector.tensor_scalar(half_ph[:], ph_sb[:].rearrange("p b t -> p (b t)"), 0.5, None, ALU.mult)

        w2_c = held([P, 2 * H], U8, "w2_c")
        w2_s = staged(36, "w2_s", [P, H], U8)
        nc.scalar.copy(
            out=w2_c[:].bitcast(U16).rearrange("p (b t m) -> p b t m", b=2, t=PACK),
            in_=w2_raw[:].bitcast(U16).rearrange("p (b m t) -> p b t m", b=2, t=PACK),
        )

        v_w = [[held([P, GW], U32, "v_w00"), held([P, GW], U32, "v_w01")],
               [held([P, GW], U32, "v_w10"), staged(99, "v_w11", [P, GW], U32)]]
        v2_w = [staged(101, "v2_w0", [P, GW], U32), staged(103, "v2_w1", [P, GW], U32)]

        def gather_words(dst, window, lst, h):
            nc.vector.tensor_copy(dst[:], window[:].indirect(lst[:, h * GW // 16:(h + 1) * GW // 16]))

        def cast(eng, dst, src):
            if eng == "s":
                nc.scalar.copy(out=dst, in_=src)
            else:
                nc.vector.tensor_copy(out=dst, in_=src)

        w1_c = [[held([P, KP], U32, f"w1_c{a}{b}") for b in range(2)] for a in range(2)]
        w1_s = [[held([P, KP], U8, f"w1_s{a}{b}") for b in range(2)] for a in range(2)]
        w3_c = [held([P, N], U32, f"w3_c{b}") for b in range(2)]
        w3_s = [held([P, N], U8, f"w3_s{b}") for b in range(2)]

        def prep_w1(a, b, eng):
            g = staged(96 + 4 * a + 10 * b, f"w1_g{a}{b}", [P, KP * PACK], BF16)
            cast(eng, g[:].rearrange("p (t m j) -> p m t j", t=PACK, j=PACK),
                 w1_raw[a, b][:].rearrange("p j (m t) -> p m t j", t=PACK))
            nc.vector.quantize_mx(out=w1_c[a][b][:].bitcast(FP8X4), scales=w1_s[a][b][:], in_=g[:])

        def prep_w3(b, eng):
            g = staged(114 + 4 * b, f"w3_g{b}", [P, N * PACK], BF16)
            cast(eng, g[:].rearrange("p (c i j) -> p c j i", i=4, j=PACK),
                 w3_raw[b][:].rearrange("p j (c i) -> p c j i", i=4))
            nc.vector.quantize_mx(out=w3_c[b][:].bitcast(FP8X4), scales=w3_s[b][:], in_=g[:])

        def a_bank(b, s):
            return 0 if b + s == 0 else 2 if b == 1 or s == 1 else 4

        def sn_at(b, s):
            return (64 + 4 * (2 * s + b)) * 1024

        def magnitudes(b, s):
            h, c0 = divmod(s * SL, GW)
            j0 = s * SL
            mag = work.tile([P, SL * PACK], F32, name="mag", bufs=3)
            for u in range(SL // P):
                acc = psum.tile([P, PACK, P], F32, name=f"acc_b{b}{s}{u}", offset=u * BANK)
                for t in range(PACK):
                    r0 = b * KP + t * P
                    nc.tensor.matmul_mx(
                        out=acc[:, t, :],
                        lhsT=w2_c[:, 2 * r0:2 * (r0 + P)].bitcast(FP4X4),
                        lhsT_scale=w2_s[:, r0:r0 + P],
                        rhs=v2_w[h][:, c0 + u * P:c0 + (u + 1) * P].bitcast(FP8X4),
                        rhs_scale=v2_s[:, j0 + u * P:j0 + (u + 1) * P],
                        start=True, stop=True,
                    )
                nc.scalar.activation(
                    mag[:, u * KP:(u + 1) * KP].rearrange("p (n t) -> p n t", t=PACK),
                    acc[:].rearrange("p t n -> p n t"), ACT.Abs)
            return mag

        def features(b, s):
            h, c0 = divmod(s * SL, GW)
            j0 = s * SL
            sn = big.tile([P, PACK, SL], F32, name=f"sn{b}{s}", offset=sn_at(b, s))
            for u in range(2):
                acc = psum.tile([P, 2, SL], F32, name=f"acc_a{b}{s}{u}", offset=(a_bank(b, s) + u) * BANK)
                for i in range(2):
                    t = 2 * u + i
                    for a in range(2):
                        nc.tensor.matmul_mx(
                            out=acc[:, i, :],
                            lhsT=w1_c[a][b][:, t * P:(t + 1) * P].bitcast(FP8X4),
                            lhsT_scale=w1_s[a][b][:, t * P:(t + 1) * P],
                            rhs=v_w[a][h][:, c0:c0 + SL].bitcast(FP8X4),
                            rhs_scale=v_s[8 * a:P, j0:j0 + SL],
                            start=(a == 0), stop=(a == 1),
                        )
                for i in range(2):
                    t = 2 * u + i
                    nc.scalar.activation(sn[:, t, :], acc[:, i, :], ACT.Sin,
                                         bias=half_ph[:, PACK * b + t:PACK * b + t + 1], scale=0.5)
            sq = work.tile([P, SL * PACK], F32, name="sq", bufs=4)
            nc.scalar.activation(sq[:].rearrange("p (c i t) -> p c t i", i=4, t=PACK),
                                 sn[:].rearrange("p t (c i) -> p c t i", i=4), ACT.Square, scale=math.sqrt(2.0))
            mag = magnitudes(b, s)
            zb = work.tile([P, SL * PACK], BF16, name="zb", align_bytes=64)
            nc.vector.scalar_tensor_tensor(zb[:], sq[:], 1.0, mag[:], ALU.subtract, ALU.mult)
            z_c = work.tile([P, SL], U32, name="z_c", bufs=8, align_bytes=64)
            z_s = work.tile([P, SL], U8, name="z_s", bufs=8, align_bytes=64)
            nc.vector.quantize_mx(out=z_c[:].bitcast(FP8X4), scales=z_s[:], in_=zb[:])
            return z_c, z_s

        def scores(items, z, bank, y_at):
            acc = psum.tile([P, 2, SL], F32, name=f"acc_y{items[0]}", offset=bank * BANK)
            for i, (n, s) in enumerate(items):
                for b in range(2):
                    nc.tensor.matmul_mx(
                        out=acc[:, i, :],
                        lhsT=w3_c[b][:, n * P:(n + 1) * P].bitcast(FP8X4),
                        lhsT_scale=w3_s[b][:, n * P:(n + 1) * P],
                        rhs=z[b, s][0][:].bitcast(FP8X4),
                        rhs_scale=z[b, s][1][:],
                        start=(b == 0), stop=(b == 1),
                    )
            y = big.tile([P, 2, SL], F32, name=f"y{items[0]}", offset=y_at)
            nc.scalar.activation(y[:], acc[:], ACT.Copy, scale=-1.0)
            for i, (n, s) in enumerate(items):
                j0 = s * SL
                nc.vector.tensor_tensor(
                    page[n][:].indirect(list3[:, j0 // 16:(j0 + SL) // 16]),
                    y[:, i, :], wgo_sb[:, j0:j0 + SL], ALU.mult)

        nc.vector.tensor_copy(v_sg[:], tab_s[:].indirect(list1[:]))
        nc.vector.tensor_copy(v_s[:].bitcast(I32), v_sg[:].bitcast(I32))
        for a in range(2):
            for r in range(2):
                nc.gpsimd.dma_start(
                    out=v_s[8 * a + 2 + r:P:32, :].bitcast(I32),
                    in_=v_sg[16 + 8 * a + r:P:32, :].bitcast(I32),
                )
        nc.vector.tensor_copy(v2_s[:], tab2_s[:].indirect(list2[:]))
        gather_words(v_w[0][0], tab_w[0], list1, 0)
        prep_w1(0, 0, "s")
        gather_words(v_w[0][1], tab_w[0], list1, 1)
        nc.vector.tensor_copy(
            out=w2_s[:].rearrange("p (b t m) -> p b t m", b=2, t=PACK),
            in_=w2_sraw[:].rearrange("p (b m t) -> p b t m", b=2, t=PACK),
        )

        prep_w1(1, 0, "s")
        gather_words(v_w[1][0], tab_w[1], list1, 0)
        gather_words(v_w[1][1], tab_w[1], list1, 1)
        gather_words(v2_w[0], tab2_w, list2, 0)
        gather_words(v2_w[1], tab2_w, list2, 1)
        prep_w1(0, 1, "v")
        prep_w1(1, 1, "v")
        z = {}
        z[0, 0] = features(0, 0)
        z[0, 1] = features(0, 1)
        prep_w3(0, "v")
        prep_w3(1, "v")
        z[1, 0] = features(1, 0)
        for s in range(1, NS):
            if s > 1:
                z[0, s] = features(0, s)
            z[1, s] = features(1, s)
            scores([(0, s - 1), (1, s - 1)], z, a_bank(1, s), sn_at(1, s))
            if s < NS - 1:
                scores([(2, s - 1), (3, s - 1)], z, a_bank(1, s) + 1, sn_at(1, s) + 2048)
        last = NS - 1
        scores([(0, last), (1, last)], z, a_bank(1, last) + 1, sn_at(1, last) + 2048)
        scores([(2, last), (2, last - 1)], z, a_bank(1, last), sn_at(0, last))
        scores([(3, last), (3, last - 1)], z, a_bank(1, last) + 1, sn_at(0, last) + 2048)
        for n in range(N // P):
            nc.sync.dma_start(out=out[n * P:(n + 1) * P, :], in_=page[n][:])
